import numpy as np
import ml_dtypes


def mxq(x, axis, fmt="e4m3"):
    dtype, down = {"e4m3": (ml_dtypes.float8_e4m3fn, 7), "e5m2": (ml_dtypes.float8_e5m2, 14)}[fmt]
    v = np.moveaxis(np.asarray(x, np.float32).astype(ml_dtypes.bfloat16).astype(np.float64), axis, -1)
    blocks = v.reshape(v.shape[:-1] + (-1, 32))
    amax = np.abs(blocks).max(-1, keepdims=True)
    byte = np.maximum(np.where(amax > 0, np.frexp(amax)[1] - 1 + 127, 0) - down, 1)
    scale = np.exp2(byte - 127.0)
    codes = (blocks / scale).astype(np.float32).astype(dtype).astype(np.float64)
    return np.moveaxis((codes * scale).reshape(v.shape), -1, axis)


WIDE = False


def mx_kscale(k):
    if not WIDE:
        return np.ones(k)
    levels = np.array([10, -10, 5, -5, 0])
    if k % 512:
        return np.exp2(np.random.permutation(np.resize(levels, k // 32))).repeat(32)
    a = np.empty((k // 512, 16))
    for p in range(k // 512):
        a[p, :8] = np.random.permutation(np.resize(levels, 8))
        for g in range(8):
            far = levels[np.abs(levels - a[p, g]) >= 10]
            a[p, g + 8] = far[np.random.randint(len(far))]
    return np.exp2(a.ravel()).repeat(32)


def f64(x):
    return np.asarray(x).astype(np.float64)


def striped(idx):
    return np.tile(idx.reshape(-1, 16).T, (8, 1)).astype(np.uint16)


def unstriped(offs):
    return offs[:16].T.reshape(-1).astype(np.int64)


E2M1 = np.array([0.0, 0.5, 1.0, 1.5, 2.0, 3.0, 4.0, 6.0, -0.0, -0.5, -1.0, -1.5, -2.0, -3.0, -4.0, -6.0])


def pack_weight(w, fmt):
    k, n = w.shape
    w = f64(np.asarray(w, np.float32).astype(ml_dtypes.bfloat16)).reshape(k // 32, 32, n)
    amax = np.abs(w).max(1)
    if fmt == "e4m3":
        byte = np.frexp(amax)[1] - 1 + 127 - 7
    else:
        mant, ex = np.frexp(amax / 6.0)
        byte = np.where(mant > 0.5, ex, ex - 1) + 127
    byte = np.clip(np.where(amax > 0, byte, 1), 1, 254)
    scaled = (w * np.exp2(127.0 - byte)[:, None, :]).reshape(k, n).astype(np.float32)
    by_word = np.ascontiguousarray(scaled.reshape(k // 512, 128, 4, n).transpose(0, 1, 3, 2))
    if fmt == "e4m3":
        words = by_word.astype(ml_dtypes.float8_e4m3fn).view(np.uint8)
    else:
        c = by_word.astype(ml_dtypes.float4_e2m1fn).view(np.uint8) & 0xF
        words = (c[..., 0::2] | (c[..., 1::2] << 4)).reshape(k // 512, 128, 2 * n)
    return np.ascontiguousarray(words), np.ascontiguousarray(byte.astype(np.uint8).reshape(k // 512, 16, n))


def unpack_weight(words, scales, fmt):
    g, _, n = scales.shape
    words = np.ascontiguousarray(words).reshape(g, 128, n, -1)
    if fmt == "e4m3":
        vals = words.view(ml_dtypes.float8_e4m3fn).astype(np.float64)
    else:
        nib = np.empty((g, 128, n, 4), np.uint8)
        nib[..., 0::2] = words & 0xF
        nib[..., 1::2] = words >> 4
        vals = E2M1[nib]
    vals = vals * np.repeat(np.exp2(scales.astype(np.float64) - 127.0), 8, axis=1)[..., None]
    return vals.transpose(0, 1, 3, 2).reshape(g * 512, n)


def gelu(v):
    return 0.5 * v * (1.0 + np.tanh(np.sqrt(2.0 / np.pi) * (v + 0.044715 * v**3)))


def bf(x):
    return np.asarray(x, np.float32).astype(ml_dtypes.bfloat16)


def planes(Y):
    n, m = Y.shape
    b = f64(bf(Y)).reshape(n // 32, 32, m)
    amax = np.abs(b).max(1)
    byte = np.clip(np.where(amax > 0, np.frexp(amax)[1] - 1 + 127 - 7, 1), 1, 254)
    codes = (b * np.exp2(127.0 - byte)[:, None, :]).reshape(n, m).astype(np.float32).astype(ml_dtypes.float8_e4m3fn).view(np.uint8)
    words = codes.reshape(n // 512, 128, 4, m).transpose(0, 1, 3, 2)
    return np.ascontiguousarray(words), np.ascontiguousarray(byte.astype(np.uint8).reshape(n // 512, 16, m))


K, H, N, T, S, P = 512, 1024, 512, 2048, 1024, 512

def setup_inputs():
    n = np.random.standard_normal
    s = mx_kscale(K)[:, None]
    u = mx_kscale(H)[:, None]
    tab_words, tab_scales = pack_weight(n((K, T)) * s, "e4m3")
    w1_words, w1_scales = pack_weight(n((K, H)) / np.sqrt(K) / s * u.T, "e2m1")
    w2 = n((K, H)) / np.sqrt(K) / s * u.T
    w3 = n((K, H)) / np.sqrt(K) / s * u.T
    wa_words, wa_scales = pack_weight(0.6 * n((H, N)) / np.sqrt(H) / u, "e4m3")
    wb = 0.7 * n((H, N)) / np.sqrt(H) / u
    amp = np.exp(0.8 * n(N))
    sign = np.where(n(N) > 0, 1.0, -1.0)
    return {
        "tab_words": tab_words, "tab_scales": tab_scales,
        "offs": striped(np.random.permutation(T)[:S]),
        "pos1": striped(np.random.permutation(S)[:P]),
        "pos2": striped(np.random.permutation(S)[:P]),
        "w1_words": w1_words, "w1_scales": w1_scales,
        "w2": w2.astype(np.float32), "w3": w3.astype(np.float32),
        "wa_words": wa_words, "wa_scales": wa_scales,
        "wb": wb.astype(np.float32),
        "temp": np.random.uniform(0.4, 1.6, N).astype(np.float32),
        "ga": (sign * np.random.uniform(3.0, 6.0, N) * amp).astype(np.float32),
        "gc": (np.random.uniform(0.6, 1.4, N) * amp).astype(np.float32),
    }

def reference(tab_words, tab_scales, offs, pos1, pos2, w1_words, w1_scales, w2, w3, wa_words, wa_scales, wb, temp, ga, gc):
    v = unpack_weight(tab_words, tab_scales, "e4m3")[:, unstriped(offs)]
    w1 = unpack_weight(w1_words, w1_scales, "e2m1")
    load1 = w1.T @ v
    load2 = mxq(f64(w2), 0, "e4m3").T @ v
    relief = mxq(f64(w3), 0, "e4m3").T @ v
    h = np.maximum(load1, load2) - relief
    hq = mxq(h, 0, "e4m3")
    wa = unpack_weight(wa_words, wa_scales, "e4m3")
    e = wa.T @ hq
    d = mxq(f64(wb), 0, "e4m3").T @ hq
    top = e.max(axis=1)
    a = np.exp(f64(temp)[:, None] * (e[:, unstriped(pos1)] - top[:, None]))
    c = d[:, unstriped(pos2)]
    y = np.maximum(f64(ga)[:, None] * a, f64(gc)[:, None] * c)
    words, scales = planes(y)
    return y, words, scales

@@ -1,0 +1,304 @@
+from contextlib import ExitStack
+
+import concourse.mybir as mybir
+
+K, H, N, T, S, P_OUT = 512, 1024, 512, 2048, 1024, 512
+FLOPS = 2 * 3 * K * H * S + 2 * 2 * H * N * S
+
+F32 = mybir.dt.float32
+BF16 = mybir.dt.bfloat16
+I32 = mybir.dt.int32
+U32 = mybir.dt.uint32
+U16 = mybir.dt.uint16
+U8 = mybir.dt.uint8
+E4M3 = mybir.dt.float8_e4m3fn_x4
+E2M1 = mybir.dt.float4_e2m1fn_x4
+ALU = mybir.AluOpType
+ACT = mybir.ActivationFunctionType
+
+P = 128
+PACK = 4
+PASS = P * PACK
+JC = 128
+QC = 256
+M_FIRST = 384
+LEAD = 5.5
+
+
+def tile_list_dock_door_desk_kernel(
+    tc, tab_words, tab_scales, offs, pos1, pos2, w1_words, w1_scales, w2, w3,
+    wa_words, wa_scales, wb, temp, ga, gc, out_0, out_1, out_2,
+):
+    nc = tc.nc
+    with ExitStack() as ctx:
+        keep = ctx.enter_context(tc.tile_pool(name="keep", bufs=1))
+        ring = ctx.enter_context(tc.tile_pool(name="ring", bufs=3))
+        psum = ctx.enter_context(tc.psum_pool(name="psum", bufs=8))
+
+        def held(name, shape, dtype):
+            return keep.tile(shape, dtype, name=name, align_bytes=64)
+
+        offs_t = held("offs_t", [P, S // 16], U16)
+        pos1_t = held("pos1_t", [P, P_OUT // 16], U16)
+        pos2_t = held("pos2_t", [P, P_OUT // 16], U16)
+        tab_w = held("tab_w", [P, T], I32)
+        tab_s = held("tab_s", [P, T], U8)
+        v_w = held("v_w", [P, S], U32)
+        v_s = held("v_s", [P, S], U8)
+        w1_raw = held("w1_raw", [P, 2 * H], U8)
+        w1_sraw = held("w1_sraw", [P, H], U8)
+        w1_c = held("w1_c", [P, 2 * H], U8)
+        w1_s = held("w1_s", [P, H], U8)
+        wa_raw = held("wa_raw", [P, 2 * N], I32)
+        wa_sraw = held("wa_sraw", [P, 2 * N], U8)
+        wa_c = held("wa_c", [P, 2 * N], I32)
+        wa_s = held("wa_s", [P, 2 * N], U8)
+        names = ("w2", "w3", "wb")
+        raw = {(n, g): held(n + "_raw%d" % g, [P, PACK, PASS], F32) for n in names for g in range(2)}
+        rounded = {(n, g): held(n + "_bf%d" % g, [P, PACK * PASS], BF16) for n in names for g in range(2)}
+        codes = {n: held(n + "_c", [P, 2 * PASS], U32) for n in names}
+        scales = {n: held(n + "_s", [P, 2 * PASS], U8) for n in names}
+        h_c = [held("h_c%d" % b, [P, S], U32) for b in range(2)]
+        h_s = [held("h_s%d" % b, [P, S], U8) for b in range(2)]
+        e_t = [held("e%d" % t, [P, S], F32) for t in range(PACK)]
+        d_t = [held("d%d" % t, [P, S], F32) for t in range(PACK)]
+        temp_t = held("temp_t", [P, PACK], F32)
+        ntemp_t = held("ntemp_t", [P, PACK], F32)
+        ga_t = held("ga_t", [P, PACK], F32)
+        gc_t = held("gc_t", [P, PACK], F32)
+        gc_wide = held("gc_wide", [P, PACK, M_FIRST], F32)
+        top = held("top", [P, S // QC, PACK], F32)
+        bias_t = held("bias_t", [P, PACK], F32)
+        y_c = held("y_c", [P, P_OUT], I32)
+        y_s = held("y_s", [P, P_OUT], U8)
+
+        def load_scale_rows(queue, tile, rows):
+            for q in range(4):
+                queue.dma_start(out=tile[32 * q : 32 * q + 4, :].bitcast(I32), in_=rows(q))
+
+        def load_weight(n, g):
+            if n == "wb":
+                src = wb[g * PASS : (g + 1) * PASS, :]
+            else:
+                src = (w2 if n == "w2" else w3)[:, g * PASS : (g + 1) * PASS]
+            nc.sync.dma_start(out=raw[n, g][:], in_=src.rearrange("(p i) c -> p i c", i=PACK))
+
+        for plane in (tab_s, w1_sraw, wa_sraw):
+            nc.gpsimd.memset(plane[:].bitcast(I32), 0)
+        nc.sync.dma_start(out=tab_w[:], in_=tab_words[0].rearrange("p c i -> p (c i)").bitcast(I32))
+        load_scale_rows(nc.sync, tab_s, lambda q: tab_scales[0, 4 * q : 4 * q + 4, :].bitcast(I32))
+        nc.sync.dma_start(offs_t[:], offs)
+        load_weight("w2", 0)
+        nc.sync.dma_start(out=w1_raw[:].bitcast(I32), in_=w1_words[0].bitcast(I32))
+        load_scale_rows(nc.sync, w1_sraw, lambda q: w1_scales[0, 4 * q : 4 * q + 4, :].bitcast(I32))
+        load_weight("w3", 0)
+        load_weight("w2", 1)
+        load_weight("w3", 1)
+        load_weight("wb", 0)
+        load_weight("wb", 1)
+        nc.sync.dma_start(
+            out=wa_raw[:].rearrange("p (a c) -> p a c", a=2),
+            in_=wa_words.rearrange("a p c i -> p a (c i)").bitcast(I32),
+        )
+        for q in range(4):
+            nc.sync.dma_start(
+                out=wa_sraw[32 * q : 32 * q + 4, :].bitcast(I32).rearrange("r (a c) -> r a c", a=2),
+                in_=wa_scales[:, 4 * q : 4 * q + 4, :].bitcast(I32).rearrange("a r c -> r a c"),
+            )
+        nc.sync.dma_start(pos1_t[:], pos1)
+        nc.sync.dma_start(pos2_t[:], pos2)
+        for tile, vec in ((temp_t, temp), (ga_t, ga), (gc_t, gc)):
+            nc.sync.dma_start(out=tile[:], in_=vec.rearrange("(p t) -> p t", t=PACK))
+
+        def gather_table(half):
+            cols = slice(half * PASS, (half + 1) * PASS)
+            part = offs_t[:, half * PASS // 16 : (half + 1) * PASS // 16]
+            nc.vector.tensor_copy(out=v_w[:, cols], in_=tab_w[:].bitcast(U32).indirect(part))
+            nc.vector.tensor_copy(out=v_s[:, cols], in_=tab_s[:].indirect(part))
+
+        def deal(ap):
+            return ap.rearrange("p (g t q) -> p g q t", g=2, t=PACK)
+
+        def undealt(ap):
+            return ap.rearrange("p (g q t) -> p g q t", g=2, t=PACK)
+
+        def round_weight(engine, n, g, q0, q1):
+            src = raw[n, g][:].rearrange("p i (q t) -> p q i t", t=PACK)[:, q0:q1]
+            dst = rounded[n, g][:].rearrange("p (t q i) -> p q i t", t=PACK, i=PACK)[:, q0:q1]
+            if engine == "scalar":
+                nc.scalar.copy(out=dst, in_=src)
+            else:
+                nc.vector.tensor_copy(out=dst, in_=src)
+
+        def quantise_weight(n, g):
+            cols = slice(g * PASS, (g + 1) * PASS)
+            nc.vector.quantize_mx(out=codes[n][:, cols].bitcast(E4M3), scales=scales[n][:, cols], in_=rounded[n, g][:])
+
+        def first_product(which, b, jc):
+            bank = psum.tile([P, PACK * JC], F32, name="bank")
+            js = slice(jc * JC, (jc + 1) * JC)
+            for t in range(PACK):
+                c0 = b * PASS + t * P
+                if which == "w1":
+                    lhs, lhs_s = w1_c[:, 2 * c0 : 2 * (c0 + P)].bitcast(E2M1), w1_s[:, c0 : c0 + P]
+                else:
+                    lhs, lhs_s = codes[which][:, c0 : c0 + P].bitcast(E4M3), scales[which][:, c0 : c0 + P]
+                nc.tensor.matmul_mx(
+                    out=bank[:, t * JC : (t + 1) * JC], lhsT=lhs, lhsT_scale=lhs_s,
+                    rhs=v_w[:, js].bitcast(E4M3), rhs_scale=v_s[:, js], start=True, stop=True,
+                )
+            return bank[:].rearrange("p (t j) -> p j t", t=PACK)
+
+        def woven(ap):
+            return ap.rearrange("p (j t) -> p j t", t=PACK)
+
+        h_bf = {}
+
+        def stronger(b, jc):
+            load1 = ring.tile([P, PACK * JC], F32, name="load1")
+            nc.scalar.activation(out=woven(load1[:]), in_=first_product("w1", b, jc), func=ACT.Copy)
+            best = ring.tile([P, PACK * JC], F32, name="best")
+            nc.vector.tensor_tensor(out=woven(best[:]), in0=first_product("w2", b, jc), in1=woven(load1[:]), op=ALU.max)
+            return best
+
+        def less_relief(b, jc, best):
+            c, part = divmod(jc, QC // JC)
+            if part == 0:
+                h_bf[b, c] = ring.tile([P, PACK * QC], BF16, name="h_bf", align_bytes=64, bufs=4)
+            dst = h_bf[b, c][:, part * PACK * JC : (part + 1) * PACK * JC]
+            nc.vector.tensor_tensor(out=woven(dst), in0=woven(best[:]), in1=first_product("w3", b, jc), op=ALU.subtract)
+
+        def quantise_h(b, c):
+            cols = slice(c * QC, (c + 1) * QC)
+            nc.vector.quantize_mx(out=h_c[b][:, cols].bitcast(E4M3), scales=h_s[b][:, cols], in_=h_bf[b, c][:])
+
+        def second_product(which, c, pair):
+            bank = psum.tile([P, PACK * JC], F32, name="bank")
+            cols = slice(c * QC, (c + 1) * QC)
+            w_c, w_s = (wa_c, wa_s) if which == "e" else (codes["wb"], scales["wb"])
+            for u in range(2):
+                for a in range(2):
+                    c0 = a * PASS + (2 * pair + u) * P
+                    nc.tensor.matmul_mx(
+                        out=bank[:, u * QC : (u + 1) * QC],
+                        lhsT=w_c[:, c0 : c0 + P].bitcast(E4M3), lhsT_scale=w_s[:, c0 : c0 + P],
+                        rhs=h_c[a][:, cols].bitcast(E4M3), rhs_scale=h_s[a][:, cols],
+                        start=(a == 0), stop=(a == 1),
+                    )
+            for u in range(2):
+                t = 2 * pair + u
+                src = bank[:, u * QC : (u + 1) * QC]
+                if which == "e":
+                    so_far = None if c == 0 else top[:, c - 1, t : t + 1]
+                    nc.vector.tensor_scalar(
+                        out=e_t[t][:, cols], in0=src, scalar1=1.0, scalar2=so_far,
+                        op0=ALU.mult, op1=ALU.max, accum_out=top[:, c, t : t + 1],
+                    )
+                else:
+                    nc.scalar.activation(out=d_t[t][:, cols], in_=src, func=ACT.Copy)
+
+        gather_table(0)
+        nc.scalar.copy(out=deal(w1_c[:].bitcast(U16)), in_=undealt(w1_raw[:].bitcast(U16)))
+        nc.vector.tensor_copy(out=deal(w1_s[:]), in_=undealt(w1_sraw[:]))
+        gather_table(1)
+        round_weight("scalar", "w2", 0, 0, 96)
+        round_weight("vector", "w2", 0, 96, 128)
+        quantise_weight("w2", 0)
+        round_weight("scalar", "w3", 0, 0, 64)
+        round_weight("vector", "w3", 0, 64, 128)
+        quantise_weight("w3", 0)
+        for g in range(2):
+            nc.gpsimd.tensor_copy(out=deal(wa_s[:])[:, g], in_=undealt(wa_sraw[:])[:, g])
+        nc.gpsimd.tensor_scalar(out=ntemp_t[:], in0=temp_t[:], scalar1=-1.0, scalar2=0.0, op0=ALU.mult, op1=ALU.add)
+        for t in range(PACK):
+            nc.gpsimd.tensor_copy(out=gc_wide[:, t, :], in_=gc_t[:, t : t + 1].to_broadcast([P, M_FIRST]))
+
+        steps = sorted(((b, jc) for b in range(2) for jc in range(S // JC)), key=lambda s: s[1] + LEAD * s[0])
+        side = [(n, g, q0) for n, g in (("w2", 1), ("w3", 1), ("wb", 0), ("wb", 1)) for q0 in range(0, P, 32)]
+        later = []
+        before = None
+        for k, (b, jc) in enumerate(steps):
+            best = stronger(b, jc)
+            for job in side[2 * k : 2 * k + 2]:
+                round_weight("scalar", job[0], job[1], job[2], job[2] + 32)
+            if k == 2:
+                quantise_weight("w2", 1)
+            if k == 4:
+                quantise_weight("w3", 1)
+            if k in (7, 9):
+                quantise_weight("wb", (k - 7) // 2)
+            if k == 8:
+                nc.scalar.copy(out=deal(wa_c[:].bitcast(U32)), in_=undealt(wa_raw[:].bitcast(U32)))
+            todo, later = later[:2], later[2:]
+            for job in todo:
+                second_product(*job)
+            if before is not None:
+                less_relief(*before)
+            if k >= 2 and steps[k - 2][1] % 2 == 1:
+                b2, jc2 = steps[k - 2]
+                quantise_h(b2, jc2 // 2)
+                if b2 == 1:
+                    later.extend((which, jc2 // 2, pair) for pair in range(2) for which in ("e", "d"))
+            before = (b, jc, best)
+        less_relief(*before)
+        for job in later:
+            second_product(*job)
+        last = S // QC - 1
+        quantise_h(1, last)
+        for pair in range(2):
+            for which in ("e", "d"):
+                second_product(which, last, pair)
+
+        out_rows = out_0.rearrange("(p t) m -> p t m", t=PACK)
+        out_words = out_1[0].rearrange("p m t -> p (m t)").bitcast(I32)
+        doors = [held("doors%d" % t, [P, P_OUT], F32) for t in range(PACK)]
+        for t in range(PACK):
+            col = slice(t, t + 1)
+            nc.scalar.activation(out=bias_t[:, col], in_=top[:, last, col], func=ACT.Copy, scale=ntemp_t[:, col])
+            nc.scalar.activation(
+                out=doors[t][:], in_=e_t[t][:].indirect(pos1_t[:]), func=ACT.Exp,
+                bias=bias_t[:, col], scale=temp_t[:, col],
+            )
+
+        def lanes_of(t, m0, m1):
+            lanes = ring.tile([P, m1 - m0], F32, name="lanes")
+            nc.vector.tensor_tensor(
+                out=lanes[:], in0=d_t[t][:].indirect(pos2_t[:, m0 // 16 : m1 // 16]),
+                in1=gc_wide[:, t, : m1 - m0], op=ALU.mult,
+            )
+            return lanes
+
+        parts = ((0, M_FIRST), (M_FIRST, P_OUT))
+        jobs = [(t, m0, m1) for m0, m1 in parts for t in range(PACK)]
+        y = {m0: held("y%d" % m0, [P, PACK, m1 - m0], F32) for m0, m1 in parts}
+        y_bf = {m0: held("y_bf%d" % m0, [P, PACK * (m1 - m0)], BF16) for m0, m1 in parts}
+
+        def weave(m0, m1):
+            nc.sync.dma_start(out=out_rows[:, :, m0:m1], in_=y[m0][:])
+            src = y[m0][:].rearrange("p t (c i) -> p c t i", i=4)
+            dst = y_bf[m0][:].rearrange("p (c i t) -> p c t i", i=4, t=PACK)
+            if m0 == 0:
+                nc.scalar.copy(out=dst, in_=src)
+            else:
+                nc.vector.tensor_copy(out=dst, in_=src)
+
+        def planes(m0, m1):
+            nc.vector.quantize_mx(out=y_c[:, m0:m1].bitcast(E4M3), scales=y_s[:, m0:m1], in_=y_bf[m0][:])
+            nc.sync.dma_start(out=out_words[:, m0:m1], in_=y_c[:, m0:m1])
+
+        ahead = lanes_of(*jobs[0])
+        for n, (t, m0, m1) in enumerate(jobs):
+            lanes = ahead
+            if n + 1 < len(jobs):
+                ahead = lanes_of(*jobs[n + 1])
+            nc.vector.scalar_tensor_tensor(
+                out=y[m0][:, t, :], in0=doors[t][:, m0:m1], scalar=ga_t[:, t : t + 1], in1=lanes[:],
+                op0=ALU.mult, op1=ALU.max,
+            )
+            if t == PACK - 1:
+                weave(m0, m1)
+        for m0, m1 in parts:
+            planes(m0, m1)
+        for q in range(4):
+            queue = nc.sync if q % 2 else nc.scalar
+            queue.dma_start(out=out_2[0, 4 * q : 4 * q + 4, :].bitcast(I32), in_=y_s[32 * q : 32 * q + 4, :].bitcast(I32))

@@ -22,7 +22,7 @@ PASS = P * PACK
 JC = 128
 QC = 256
 M_FIRST = 384
-LEAD = 5.5
+LEAD = 2.5
 
 
 def tile_list_dock_door_desk_kernel(
@@ -33,7 +33,7 @@ def tile_list_dock_door_desk_kernel(
     with ExitStack() as ctx:
         keep = ctx.enter_context(tc.tile_pool(name="keep", bufs=1))
         ring = ctx.enter_context(tc.tile_pool(name="ring", bufs=3))
-        psum = ctx.enter_context(tc.psum_pool(name="psum", bufs=8))
+        psum = ctx.enter_context(tc.psum_pool(name="psum", bufs=2))
 
         def held(name, shape, dtype):
             return keep.tile(shape, dtype, name=name, align_bytes=64)
@@ -54,7 +54,12 @@ def tile_list_dock_door_desk_kernel(
         wa_c = held("wa_c", [P, 2 * N], I32)
         wa_s = held("wa_s", [P, 2 * N], U8)
         names = ("w2", "w3", "wb")
-        raw = {(n, g): held(n + "_raw%d" % g, [P, PACK, PASS], F32) for n in names for g in range(2)}
+        raw = {
+            (n, g, u): held(n + "_raw%d%d" % (g, u), [P, PACK, PASS // 2], F32)
+            for n in names[:2] for g in range(1) for u in range(2)
+        }
+        for n, g in (("w2", 1), ("w3", 1), ("wb", 0), ("wb", 1)):
+            raw[n, g] = held(n + "_raw%d" % g, [P, PACK, PASS], F32)
         rounded = {(n, g): held(n + "_bf%d" % g, [P, PACK * PASS], BF16) for n in names for g in range(2)}
         codes = {n: held(n + "_c", [P, 2 * PASS], U32) for n in names}
         scales = {n: held(n + "_s", [P, 2 * PASS], U8) for n in names}
@@ -83,19 +88,23 @@ def tile_list_dock_door_desk_kernel(
                 src = (w2 if n == "w2" else w3)[:, g * PASS : (g + 1) * PASS]
             nc.sync.dma_start(out=raw[n, g][:], in_=src.rearrange("(p i) c -> p i c", i=PACK))
 
+        def load_half(n, u):
+            src = (w2 if n == "w2" else w3)[:, u * PASS // 2 : (u + 1) * PASS // 2]
+            nc.sync.dma_start(out=raw[n, 0, u][:], in_=src.rearrange("(p i) c -> p i c", i=PACK))
+
         for plane in (tab_s, w1_sraw, wa_sraw):
             nc.gpsimd.memset(plane[:].bitcast(I32), 0)
+        nc.sync.dma_start(offs_t[:], offs)
         nc.sync.dma_start(out=tab_w[:], in_=tab_words[0].rearrange("p c i -> p (c i)").bitcast(I32))
         load_scale_rows(nc.sync, tab_s, lambda q: tab_scales[0, 4 * q : 4 * q + 4, :].bitcast(I32))
-        nc.sync.dma_start(offs_t[:], offs)
-        load_weight("w2", 0)
+        load_half("w2", 0)
+        load_half("w2", 1)
         nc.sync.dma_start(out=w1_raw[:].bitcast(I32), in_=w1_words[0].bitcast(I32))
+        load_half("w3", 0)
         load_scale_rows(nc.sync, w1_sraw, lambda q: w1_scales[0, 4 * q : 4 * q + 4, :].bitcast(I32))
-        load_weight("w3", 0)
+        load_half("w3", 1)
         load_weight("w2", 1)
         load_weight("w3", 1)
-        load_weight("wb", 0)
-        load_weight("wb", 1)
         nc.sync.dma_start(
             out=wa_raw[:].rearrange("p (a c) -> p a c", a=2),
             in_=wa_words.rearrange("a p c i -> p a (c i)").bitcast(I32),
@@ -105,6 +114,8 @@ def tile_list_dock_door_desk_kernel(
                 out=wa_sraw[32 * q : 32 * q + 4, :].bitcast(I32).rearrange("r (a c) -> r a c", a=2),
                 in_=wa_scales[:, 4 * q : 4 * q + 4, :].bitcast(I32).rearrange("a r c -> r a c"),
             )
+        load_weight("wb", 0)
+        load_weight("wb", 1)
         nc.sync.dma_start(pos1_t[:], pos1)
         nc.sync.dma_start(pos2_t[:], pos2)
         for tile, vec in ((temp_t, temp), (ga_t, ga), (gc_t, gc)):
@@ -122,8 +133,20 @@ def tile_list_dock_door_desk_kernel(
         def undealt(ap):
             return ap.rearrange("p (g q t) -> p g q t", g=2, t=PACK)
 
+        def deal_scales(dst, src):
+            for g in range(2):
+                cols = slice(g * PASS, (g + 1) * PASS)
+                nc.gpsimd.tensor_copy(
+                    out=dst[:, cols].rearrange("p (t q) -> p t q", t=PACK),
+                    in_=src[:, cols].rearrange("p (q t) -> p t q", t=PACK),
+                )
+
         def round_weight(engine, n, g, q0, q1):
-            src = raw[n, g][:].rearrange("p i (q t) -> p q i t", t=PACK)[:, q0:q1]
+            if (n, g) in raw:
+                src = raw[n, g][:].rearrange("p i (q t) -> p q i t", t=PACK)[:, q0:q1]
+            else:
+                u, q = divmod(q0, P // 2)
+                src = raw[n, g, u][:].rearrange("p i (q t) -> p q i t", t=PACK)[:, q : q + q1 - q0]
             dst = rounded[n, g][:].rearrange("p (t q i) -> p q i t", t=PACK, i=PACK)[:, q0:q1]
             if engine == "scalar":
                 nc.scalar.copy(out=dst, in_=src)
@@ -135,7 +158,7 @@ def tile_list_dock_door_desk_kernel(
             nc.vector.quantize_mx(out=codes[n][:, cols].bitcast(E4M3), scales=scales[n][:, cols], in_=rounded[n, g][:])
 
         def first_product(which, b, jc):
-            bank = psum.tile([P, PACK * JC], F32, name="bank")
+            bank = psum.tile([P, PACK * JC], F32, name="bank_" + which)
             js = slice(jc * JC, (jc + 1) * JC)
             for t in range(PACK):
                 c0 = b * PASS + t * P
@@ -161,19 +184,24 @@ def tile_list_dock_door_desk_kernel(
             nc.vector.tensor_tensor(out=woven(best[:]), in0=first_product("w2", b, jc), in1=woven(load1[:]), op=ALU.max)
             return best
 
-        def less_relief(b, jc, best):
+        def less_relief(k, b, jc, best):
             c, part = divmod(jc, QC // JC)
             if part == 0:
                 h_bf[b, c] = ring.tile([P, PACK * QC], BF16, name="h_bf", align_bytes=64, bufs=4)
             dst = h_bf[b, c][:, part * PACK * JC : (part + 1) * PACK * JC]
-            nc.vector.tensor_tensor(out=woven(dst), in0=woven(best[:]), in1=first_product("w3", b, jc), op=ALU.subtract)
+            if k >= 99 and part == 1:
+                relief = ring.tile([P, PACK * JC], F32, name="relief")
+                nc.scalar.activation(out=woven(relief[:]), in_=first_product("w3", b, jc), func=ACT.Copy)
+                nc.gpsimd.tensor_tensor(out=dst, in0=best[:], in1=relief[:], op=ALU.subtract)
+            else:
+                nc.vector.tensor_tensor(out=woven(dst), in0=woven(best[:]), in1=first_product("w3", b, jc), op=ALU.subtract)
 
         def quantise_h(b, c):
             cols = slice(c * QC, (c + 1) * QC)
             nc.vector.quantize_mx(out=h_c[b][:, cols].bitcast(E4M3), scales=h_s[b][:, cols], in_=h_bf[b, c][:])
 
-        def second_product(which, c, pair):
-            bank = psum.tile([P, PACK * JC], F32, name="bank")
+        def second_product(which, c, pair, tag="second"):
+            bank = psum.tile([P, PACK * JC], F32, name="bank_" + tag)
             cols = slice(c * QC, (c + 1) * QC)
             w_c, w_s = (wa_c, wa_s) if which == "e" else (codes["wb"], scales["wb"])
             for u in range(2):
@@ -198,56 +226,73 @@ def tile_list_dock_door_desk_kernel(
                     nc.scalar.activation(out=d_t[t][:, cols], in_=src, func=ACT.Copy)
 
         gather_table(0)
-        nc.scalar.copy(out=deal(w1_c[:].bitcast(U16)), in_=undealt(w1_raw[:].bitcast(U16)))
+        round_weight("scalar", "w2", 0, 0, 64)
+        round_weight("scalar", "w2", 0, 64, 128)
+        quantise_weight("w2", 0)
+        nc.scalar.copy(out=deal(w1_c[:].bitcast(U16))[:, 0], in_=undealt(w1_raw[:].bitcast(U16))[:, 0])
         nc.vector.tensor_copy(out=deal(w1_s[:]), in_=undealt(w1_sraw[:]))
         gather_table(1)
-        round_weight("scalar", "w2", 0, 0, 96)
-        round_weight("vector", "w2", 0, 96, 128)
-        quantise_weight("w2", 0)
         round_weight("scalar", "w3", 0, 0, 64)
         round_weight("vector", "w3", 0, 64, 128)
         quantise_weight("w3", 0)
-        for g in range(2):
-            nc.gpsimd.tensor_copy(out=deal(wa_s[:])[:, g], in_=undealt(wa_sraw[:])[:, g])
+        deal_scales(wa_s, wa_sraw)
         nc.gpsimd.tensor_scalar(out=ntemp_t[:], in0=temp_t[:], scalar1=-1.0, scalar2=0.0, op0=ALU.mult, op1=ALU.add)
-        for t in range(PACK):
-            nc.gpsimd.tensor_copy(out=gc_wide[:, t, :], in_=gc_t[:, t : t + 1].to_broadcast([P, M_FIRST]))
 
-        steps = sorted(((b, jc) for b in range(2) for jc in range(S // JC)), key=lambda s: s[1] + LEAD * s[0])
-        side = [(n, g, q0) for n, g in (("w2", 1), ("w3", 1), ("wb", 0), ("wb", 1)) for q0 in range(0, P, 32)]
-        later = []
+        steps = sorted(((b, jc) for b in range(2) for jc in range(S // JC)), key=lambda s: s[1] // 2 + LEAD * s[0])
+        side = [
+            (n, g, 2 * (u * P // 2 // pieces), 2 * ((u + 1) * P // 2 // pieces))
+            for n, g, pieces in (("w2", 1, 2), ("w3", 1, 2), ("wb", 0, 3), ("wb", 1, 3))
+            for u in range(pieces)
+        ]
+        per_step = [1,1,1,1,1,1,1,1,1,1]
+        rounded_so_far = 0
+        quantised = set()
+        ready_chunks = []
+        made = set()
         before = None
+
+        def second_stage(budget):
+            for c in ready_chunks:
+                for pair in range(2):
+                    for which in ("e", "d"):
+                        if budget and (which, c, pair) not in made and (which == "e" or ("wb", 1) in quantised):
+                            made.add((which, c, pair))
+                            second_product(which, c, pair)
+                            budget -= 1
+
         for k, (b, jc) in enumerate(steps):
             best = stronger(b, jc)
-            for job in side[2 * k : 2 * k + 2]:
-                round_weight("scalar", job[0], job[1], job[2], job[2] + 32)
-            if k == 2:
-                quantise_weight("w2", 1)
+            done_before = side[:rounded_so_far]
+            count = per_step[k] if k < len(per_step) else 0
+            for job in side[rounded_so_far : rounded_so_far + count]:
+                round_weight("scalar", job[0], job[1], job[2], job[3])
+            rounded_so_far += count
+            if k == 1:
+                nc.scalar.copy(out=deal(w1_c[:].bitcast(U16))[:, 1], in_=undealt(w1_raw[:].bitcast(U16))[:, 1])
             if k == 4:
-                quantise_weight("w3", 1)
-            if k in (7, 9):
-                quantise_weight("wb", (k - 7) // 2)
-            if k == 8:
-                nc.scalar.copy(out=deal(wa_c[:].bitcast(U32)), in_=undealt(wa_raw[:].bitcast(U32)))
-            todo, later = later[:2], later[2:]
-            for job in todo:
-                second_product(*job)
+                deal_scales(wa_c, wa_raw)
+            if k == 12:
+                nc.scalar.copy(out=gc_wide[:], in_=gc_t[:].unsqueeze(2).to_broadcast([P, PACK, M_FIRST]))
+            second_stage(3)
             if before is not None:
                 less_relief(*before)
             if k >= 2 and steps[k - 2][1] % 2 == 1:
                 b2, jc2 = steps[k - 2]
                 quantise_h(b2, jc2 // 2)
                 if b2 == 1:
-                    later.extend((which, jc2 // 2, pair) for pair in range(2) for which in ("e", "d"))
-            before = (b, jc, best)
+                    ready_chunks.append(jc2 // 2)
+            for n, g, q0, q1 in done_before:
+                if q1 == P and (n, g) not in quantised:
+                    quantised.add((n, g))
+                    quantise_weight(n, g)
+            before = (k, b, jc, best)
         less_relief(*before)
-        for job in later:
-            second_product(*job)
+        second_stage(16)
         last = S // QC - 1
         quantise_h(1, last)
         for pair in range(2):
             for which in ("e", "d"):
-                second_product(which, last, pair)
+                second_product(which, last, pair, "w2" if which == "e" else "w1")
 
         out_rows = out_0.rearrange("(p t) m -> p t m", t=PACK)
         out_words = out_1[0].rearrange("p m t -> p (m t)").bitcast(I32)

@@ -2,7 +2,7 @@ from contextlib import ExitStack
 
 import concourse.mybir as mybir
 
-K, H, N, T, S, P_OUT = 512, 1024, 512, 2048, 1024, 512
+K, H, N, T, S, M = 512, 1024, 512, 2048, 1024, 512
 FLOPS = 2 * 3 * K * H * S + 2 * 2 * H * N * S
 
 F32 = mybir.dt.float32
@@ -19,10 +19,16 @@ ACT = mybir.ActivationFunctionType
 P = 128
 PACK = 4
 PASS = P * PACK
-JC = 128
-QC = 256
-M_FIRST = 384
+PER_COLUMN = 16
+STEP = 128
+CHUNK = 2 * STEP
+CHUNKS = S // CHUNK
 LEAD = 2.5
+PIECES_FIRST_STAGE = 2
+PIECES_WB = 3
+GPSIMD_FROM = 8
+BANKS_PER_STEP = 3
+M_FIRST = 384
 
 
 def tile_list_dock_door_desk_kernel(
@@ -38,9 +44,9 @@ def tile_list_dock_door_desk_kernel(
         def held(name, shape, dtype):
             return keep.tile(shape, dtype, name=name, align_bytes=64)
 
-        offs_t = held("offs_t", [P, S // 16], U16)
-        pos1_t = held("pos1_t", [P, P_OUT // 16], U16)
-        pos2_t = held("pos2_t", [P, P_OUT // 16], U16)
+        offs_t = held("offs_t", [P, S // PER_COLUMN], U16)
+        pos1_t = held("pos1_t", [P, M // PER_COLUMN], U16)
+        pos2_t = held("pos2_t", [P, M // PER_COLUMN], U16)
         tab_w = held("tab_w", [P, T], I32)
         tab_s = held("tab_s", [P, T], U8)
         v_w = held("v_w", [P, S], U32)
@@ -53,87 +59,91 @@ def tile_list_dock_door_desk_kernel(
         wa_sraw = held("wa_sraw", [P, 2 * N], U8)
         wa_c = held("wa_c", [P, 2 * N], I32)
         wa_s = held("wa_s", [P, 2 * N], U8)
-        names = ("w2", "w3", "wb")
-        raw = {
-            (n, g, u): held(n + "_raw%d%d" % (g, u), [P, PACK, PASS // 2], F32)
-            for n in names[:2] for g in range(1) for u in range(2)
+        float_weights = ("w2", "w3", "wb")
+        late_groups = (("w2", 1), ("w3", 1), ("wb", 0), ("wb", 1))
+        early_raw = {
+            (n, u): held(n + "_early%d" % u, [P, PACK, PASS // 2], F32) for n in ("w2", "w3") for u in range(2)
         }
-        for n, g in (("w2", 1), ("w3", 1), ("wb", 0), ("wb", 1)):
-            raw[n, g] = held(n + "_raw%d" % g, [P, PACK, PASS], F32)
-        rounded = {(n, g): held(n + "_bf%d" % g, [P, PACK * PASS], BF16) for n in names for g in range(2)}
-        codes = {n: held(n + "_c", [P, 2 * PASS], U32) for n in names}
-        scales = {n: held(n + "_s", [P, 2 * PASS], U8) for n in names}
+        late_raw = {(n, g): held(n + "_late%d" % g, [P, PACK, PASS], F32) for n, g in late_groups}
+        rounded = {(n, g): held(n + "_bf%d" % g, [P, PACK * PASS], BF16) for n in float_weights for g in range(2)}
+        codes = {n: held(n + "_c", [P, 2 * PASS], U32) for n in float_weights}
+        scales = {n: held(n + "_s", [P, 2 * PASS], U8) for n in float_weights}
         h_c = [held("h_c%d" % b, [P, S], U32) for b in range(2)]
         h_s = [held("h_s%d" % b, [P, S], U8) for b in range(2)]
         e_t = [held("e%d" % t, [P, S], F32) for t in range(PACK)]
         d_t = [held("d%d" % t, [P, S], F32) for t in range(PACK)]
         temp_t = held("temp_t", [P, PACK], F32)
-        ntemp_t = held("ntemp_t", [P, PACK], F32)
+        minus_temp = held("minus_temp", [P, PACK], F32)
         ga_t = held("ga_t", [P, PACK], F32)
         gc_t = held("gc_t", [P, PACK], F32)
         gc_wide = held("gc_wide", [P, PACK, M_FIRST], F32)
-        top = held("top", [P, S // QC, PACK], F32)
+        top = held("top", [P, CHUNKS, PACK], F32)
         bias_t = held("bias_t", [P, PACK], F32)
-        y_c = held("y_c", [P, P_OUT], I32)
-        y_s = held("y_s", [P, P_OUT], U8)
+        y_c = held("y_c", [P, M], I32)
+        y_s = held("y_s", [P, M], U8)
 
-        def load_scale_rows(queue, tile, rows):
+        def scale_rows(plane, q):
+            return plane[32 * q : 32 * q + 4, :].bitcast(I32)
+
+        def load_scales(plane, rows):
             for q in range(4):
-                queue.dma_start(out=tile[32 * q : 32 * q + 4, :].bitcast(I32), in_=rows(q))
+                nc.sync.dma_start(out=scale_rows(plane, q), in_=rows[4 * q : 4 * q + 4, :].bitcast(I32))
 
-        def load_weight(n, g):
-            if n == "wb":
-                src = wb[g * PASS : (g + 1) * PASS, :]
-            else:
-                src = (w2 if n == "w2" else w3)[:, g * PASS : (g + 1) * PASS]
-            nc.sync.dma_start(out=raw[n, g][:], in_=src.rearrange("(p i) c -> p i c", i=PACK))
+        def load_rows(dst, src):
+            nc.sync.dma_start(out=dst[:], in_=src.rearrange("(p i) c -> p i c", i=PACK))
 
-        def load_half(n, u):
-            src = (w2 if n == "w2" else w3)[:, u * PASS // 2 : (u + 1) * PASS // 2]
-            nc.sync.dma_start(out=raw[n, 0, u][:], in_=src.rearrange("(p i) c -> p i c", i=PACK))
+        def load_early(n, u):
+            load_rows(early_raw[n, u], (w2 if n == "w2" else w3)[:, u * PASS // 2 : (u + 1) * PASS // 2])
+
+        def load_vector(dst, vec):
+            nc.sync.dma_start(out=dst[:], in_=vec.rearrange("(p t) -> p t", t=PACK))
 
         for plane in (tab_s, w1_sraw, wa_sraw):
             nc.gpsimd.memset(plane[:].bitcast(I32), 0)
+        load_vector(gc_t, gc)
         nc.sync.dma_start(offs_t[:], offs)
         nc.sync.dma_start(out=tab_w[:], in_=tab_words[0].rearrange("p c i -> p (c i)").bitcast(I32))
-        load_scale_rows(nc.sync, tab_s, lambda q: tab_scales[0, 4 * q : 4 * q + 4, :].bitcast(I32))
-        load_half("w2", 0)
-        load_half("w2", 1)
+        load_scales(tab_s, tab_scales[0])
+        load_early("w2", 0)
+        load_early("w2", 1)
         nc.sync.dma_start(out=w1_raw[:].bitcast(I32), in_=w1_words[0].bitcast(I32))
-        load_half("w3", 0)
-        load_scale_rows(nc.sync, w1_sraw, lambda q: w1_scales[0, 4 * q : 4 * q + 4, :].bitcast(I32))
-        load_half("w3", 1)
-        load_weight("w2", 1)
-        load_weight("w3", 1)
+        load_early("w3", 0)
+        load_scales(w1_sraw, w1_scales[0])
+        load_early("w3", 1)
+        load_rows(late_raw["w2", 1], w2[:, PASS:])
+        load_rows(late_raw["w3", 1], w3[:, PASS:])
         nc.sync.dma_start(
             out=wa_raw[:].rearrange("p (a c) -> p a c", a=2),
             in_=wa_words.rearrange("a p c i -> p a (c i)").bitcast(I32),
         )
         for q in range(4):
             nc.sync.dma_start(
-                out=wa_sraw[32 * q : 32 * q + 4, :].bitcast(I32).rearrange("r (a c) -> r a c", a=2),
+                out=scale_rows(wa_sraw, q).rearrange("r (a c) -> r a c", a=2),
                 in_=wa_scales[:, 4 * q : 4 * q + 4, :].bitcast(I32).rearrange("a r c -> r a c"),
             )
-        load_weight("wb", 0)
-        load_weight("wb", 1)
+        load_rows(late_raw["wb", 0], wb[:PASS, :])
+        load_rows(late_raw["wb", 1], wb[PASS:, :])
         nc.sync.dma_start(pos1_t[:], pos1)
         nc.sync.dma_start(pos2_t[:], pos2)
-        for tile, vec in ((temp_t, temp), (ga_t, ga), (gc_t, gc)):
-            nc.sync.dma_start(out=tile[:], in_=vec.rearrange("(p t) -> p t", t=PACK))
+        load_vector(temp_t, temp)
+        load_vector(ga_t, ga)
 
         def gather_table(half):
-            cols = slice(half * PASS, (half + 1) * PASS)
-            part = offs_t[:, half * PASS // 16 : (half + 1) * PASS // 16]
-            nc.vector.tensor_copy(out=v_w[:, cols], in_=tab_w[:].bitcast(U32).indirect(part))
-            nc.vector.tensor_copy(out=v_s[:, cols], in_=tab_s[:].indirect(part))
+            cols = slice(half * S // 2, (half + 1) * S // 2)
+            entries = offs_t[:, cols.start // PER_COLUMN : cols.stop // PER_COLUMN]
+            nc.vector.tensor_copy(out=v_w[:, cols], in_=tab_w[:].bitcast(U32).indirect(entries))
+            nc.vector.tensor_copy(out=v_s[:, cols], in_=tab_s[:].indirect(entries))
 
-        def deal(ap):
+        def dealt(ap):
             return ap.rearrange("p (g t q) -> p g q t", g=2, t=PACK)
 
         def undealt(ap):
             return ap.rearrange("p (g q t) -> p g q t", g=2, t=PACK)
 
-        def deal_scales(dst, src):
+        def deal_w1_words(g):
+            nc.scalar.copy(out=dealt(w1_c[:].bitcast(U16))[:, g], in_=undealt(w1_raw[:].bitcast(U16))[:, g])
+
+        def deal_on_gpsimd(dst, src):
             for g in range(2):
                 cols = slice(g * PASS, (g + 1) * PASS)
                 nc.gpsimd.tensor_copy(
@@ -141,33 +151,25 @@ def tile_list_dock_door_desk_kernel(
                     in_=src[:, cols].rearrange("p (q t) -> p t q", t=PACK),
                 )
 
-        def round_weight(engine, n, g, q0, q1):
-            if (n, g) in raw:
-                src = raw[n, g][:].rearrange("p i (q t) -> p q i t", t=PACK)[:, q0:q1]
-            else:
-                u, q = divmod(q0, P // 2)
-                src = raw[n, g, u][:].rearrange("p i (q t) -> p q i t", t=PACK)[:, q : q + q1 - q0]
+        def round_weight(copy, raw, n, g, q0, q1):
             dst = rounded[n, g][:].rearrange("p (t q i) -> p q i t", t=PACK, i=PACK)[:, q0:q1]
-            if engine == "scalar":
-                nc.scalar.copy(out=dst, in_=src)
-            else:
-                nc.vector.tensor_copy(out=dst, in_=src)
+            copy(out=dst, in_=raw.rearrange("p i (q t) -> p q i t", t=PACK))
 
         def quantise_weight(n, g):
             cols = slice(g * PASS, (g + 1) * PASS)
             nc.vector.quantize_mx(out=codes[n][:, cols].bitcast(E4M3), scales=scales[n][:, cols], in_=rounded[n, g][:])
 
-        def first_product(which, b, jc):
-            bank = psum.tile([P, PACK * JC], F32, name="bank_" + which)
-            js = slice(jc * JC, (jc + 1) * JC)
+        def first_product(n, b, step):
+            bank = psum.tile([P, PACK * STEP], F32, name="bank_" + n)
+            js = slice(step * STEP, (step + 1) * STEP)
             for t in range(PACK):
                 c0 = b * PASS + t * P
-                if which == "w1":
+                if n == "w1":
                     lhs, lhs_s = w1_c[:, 2 * c0 : 2 * (c0 + P)].bitcast(E2M1), w1_s[:, c0 : c0 + P]
                 else:
-                    lhs, lhs_s = codes[which][:, c0 : c0 + P].bitcast(E4M3), scales[which][:, c0 : c0 + P]
+                    lhs, lhs_s = codes[n][:, c0 : c0 + P].bitcast(E4M3), scales[n][:, c0 : c0 + P]
                 nc.tensor.matmul_mx(
-                    out=bank[:, t * JC : (t + 1) * JC], lhsT=lhs, lhsT_scale=lhs_s,
+                    out=bank[:, t * STEP : (t + 1) * STEP], lhsT=lhs, lhsT_scale=lhs_s,
                     rhs=v_w[:, js].bitcast(E4M3), rhs_scale=v_s[:, js], start=True, stop=True,
                 )
             return bank[:].rearrange("p (t j) -> p j t", t=PACK)
@@ -175,131 +177,129 @@ def tile_list_dock_door_desk_kernel(
         def woven(ap):
             return ap.rearrange("p (j t) -> p j t", t=PACK)
 
-        h_bf = {}
-
-        def stronger(b, jc):
-            load1 = ring.tile([P, PACK * JC], F32, name="load1")
-            nc.scalar.activation(out=woven(load1[:]), in_=first_product("w1", b, jc), func=ACT.Copy)
-            best = ring.tile([P, PACK * JC], F32, name="best")
-            nc.vector.tensor_tensor(out=woven(best[:]), in0=first_product("w2", b, jc), in1=woven(load1[:]), op=ALU.max)
+        def stronger_load(b, step):
+            load1 = ring.tile([P, PACK * STEP], F32, name="load1")
+            nc.scalar.activation(out=woven(load1[:]), in_=first_product("w1", b, step), func=ACT.Copy)
+            best = ring.tile([P, PACK * STEP], F32, name="best")
+            nc.vector.tensor_tensor(out=woven(best[:]), in0=first_product("w2", b, step), in1=woven(load1[:]), op=ALU.max)
             return best
 
-        def less_relief(k, b, jc, best):
-            c, part = divmod(jc, QC // JC)
+        h_bf = {}
+
+        def less_relief(b, step, best, on_gpsimd):
+            chunk, part = divmod(step, 2)
             if part == 0:
-                h_bf[b, c] = ring.tile([P, PACK * QC], BF16, name="h_bf", align_bytes=64, bufs=4)
-            dst = h_bf[b, c][:, part * PACK * JC : (part + 1) * PACK * JC]
-            if k >= 99 and part == 1:
-                relief = ring.tile([P, PACK * JC], F32, name="relief")
-                nc.scalar.activation(out=woven(relief[:]), in_=first_product("w3", b, jc), func=ACT.Copy)
+                h_bf[b, chunk] = ring.tile([P, PACK * CHUNK], BF16, name="h_bf", align_bytes=64, bufs=4)
+            dst = h_bf[b, chunk][:, part * PACK * STEP : (part + 1) * PACK * STEP]
+            if on_gpsimd:
+                relief = ring.tile([P, PACK * STEP], F32, name="relief")
+                nc.scalar.activation(out=woven(relief[:]), in_=first_product("w3", b, step), func=ACT.Copy)
                 nc.gpsimd.tensor_tensor(out=dst, in0=best[:], in1=relief[:], op=ALU.subtract)
             else:
-                nc.vector.tensor_tensor(out=woven(dst), in0=woven(best[:]), in1=first_product("w3", b, jc), op=ALU.subtract)
+                nc.vector.tensor_tensor(
+                    out=woven(dst), in0=woven(best[:]), in1=first_product("w3", b, step), op=ALU.subtract,
+                )
 
-        def quantise_h(b, c):
-            cols = slice(c * QC, (c + 1) * QC)
-            nc.vector.quantize_mx(out=h_c[b][:, cols].bitcast(E4M3), scales=h_s[b][:, cols], in_=h_bf[b, c][:])
+        def quantise_h(b, chunk):
+            cols = slice(chunk * CHUNK, (chunk + 1) * CHUNK)
+            nc.vector.quantize_mx(out=h_c[b][:, cols].bitcast(E4M3), scales=h_s[b][:, cols], in_=h_bf[b, chunk][:])
 
-        def second_product(which, c, pair, tag="second"):
-            bank = psum.tile([P, PACK * JC], F32, name="bank_" + tag)
-            cols = slice(c * QC, (c + 1) * QC)
+        def second_product(which, chunk, pair, tag):
+            bank = psum.tile([P, 2 * CHUNK], F32, name="bank_" + tag)
+            cols = slice(chunk * CHUNK, (chunk + 1) * CHUNK)
             w_c, w_s = (wa_c, wa_s) if which == "e" else (codes["wb"], scales["wb"])
             for u in range(2):
                 for a in range(2):
                     c0 = a * PASS + (2 * pair + u) * P
                     nc.tensor.matmul_mx(
-                        out=bank[:, u * QC : (u + 1) * QC],
+                        out=bank[:, u * CHUNK : (u + 1) * CHUNK],
                         lhsT=w_c[:, c0 : c0 + P].bitcast(E4M3), lhsT_scale=w_s[:, c0 : c0 + P],
                         rhs=h_c[a][:, cols].bitcast(E4M3), rhs_scale=h_s[a][:, cols],
                         start=(a == 0), stop=(a == 1),
                     )
             for u in range(2):
                 t = 2 * pair + u
-                src = bank[:, u * QC : (u + 1) * QC]
+                src = bank[:, u * CHUNK : (u + 1) * CHUNK]
                 if which == "e":
-                    so_far = None if c == 0 else top[:, c - 1, t : t + 1]
+                    so_far = None if chunk == 0 else top[:, chunk - 1, t : t + 1]
                     nc.vector.tensor_scalar(
                         out=e_t[t][:, cols], in0=src, scalar1=1.0, scalar2=so_far,
-                        op0=ALU.mult, op1=ALU.max, accum_out=top[:, c, t : t + 1],
+                        op0=ALU.mult, op1=ALU.max, accum_out=top[:, chunk, t : t + 1],
                     )
                 else:
                     nc.scalar.activation(out=d_t[t][:, cols], in_=src, func=ACT.Copy)
 
         gather_table(0)
-        round_weight("scalar", "w2", 0, 0, 64)
-        round_weight("scalar", "w2", 0, 64, 128)
+        round_weight(nc.scalar.copy, early_raw["w2", 0][:], "w2", 0, 0, P // 2)
+        round_weight(nc.scalar.copy, early_raw["w2", 1][:], "w2", 0, P // 2, P)
         quantise_weight("w2", 0)
-        nc.scalar.copy(out=deal(w1_c[:].bitcast(U16))[:, 0], in_=undealt(w1_raw[:].bitcast(U16))[:, 0])
-        nc.vector.tensor_copy(out=deal(w1_s[:]), in_=undealt(w1_sraw[:]))
+        deal_w1_words(0)
+        nc.vector.tensor_copy(out=dealt(w1_s[:]), in_=undealt(w1_sraw[:]))
         gather_table(1)
-        round_weight("scalar", "w3", 0, 0, 64)
-        round_weight("vector", "w3", 0, 64, 128)
+        round_weight(nc.scalar.copy, early_raw["w3", 0][:], "w3", 0, 0, P // 2)
+        round_weight(nc.vector.tensor_copy, early_raw["w3", 1][:], "w3", 0, P // 2, P)
         quantise_weight("w3", 0)
-        deal_scales(wa_s, wa_sraw)
-        nc.gpsimd.tensor_scalar(out=ntemp_t[:], in0=temp_t[:], scalar1=-1.0, scalar2=0.0, op0=ALU.mult, op1=ALU.add)
 
-        steps = sorted(((b, jc) for b in range(2) for jc in range(S // JC)), key=lambda s: s[1] // 2 + LEAD * s[0])
-        side = [
-            (n, g, 2 * (u * P // 2 // pieces), 2 * ((u + 1) * P // 2 // pieces))
-            for n, g, pieces in (("w2", 1, 2), ("w3", 1, 2), ("wb", 0, 3), ("wb", 1, 3))
-            for u in range(pieces)
-        ]
-        per_step = [1,1,1,1,1,1,1,1,1,1]
-        rounded_so_far = 0
-        quantised = set()
+        deal_on_gpsimd(wa_s, wa_sraw)
+        nc.gpsimd.tensor_scalar(out=minus_temp[:], in0=temp_t[:], scalar1=-1.0, scalar2=0.0, op0=ALU.mult, op1=ALU.add)
+        for t in range(PACK):
+            nc.gpsimd.tensor_copy(out=gc_wide[:, t, :], in_=gc_t[:, t : t + 1].to_broadcast([P, M_FIRST]))
+        deal_on_gpsimd(wa_c, wa_raw)
+
+        steps = sorted(((b, step) for b in range(2) for step in range(S // STEP)), key=lambda s: s[1] // 2 + LEAD * s[0])
+        pieces = []
+        for n, g in late_groups:
+            count = PIECES_WB if n == "wb" else PIECES_FIRST_STAGE
+            bounds = [2 * (u * P // 2 // count) for u in range(count + 1)]
+            pieces.extend((n, g, bounds[u], bounds[u + 1]) for u in range(count))
         ready_chunks = []
-        made = set()
-        before = None
+        issued = set()
 
-        def second_stage(budget):
-            for c in ready_chunks:
+        def second_stage(budget, wb_ready):
+            for chunk in ready_chunks:
                 for pair in range(2):
                     for which in ("e", "d"):
-                        if budget and (which, c, pair) not in made and (which == "e" or ("wb", 1) in quantised):
-                            made.add((which, c, pair))
-                            second_product(which, c, pair)
+                        if budget and (which, chunk, pair) not in issued and (which == "e" or wb_ready):
+                            issued.add((which, chunk, pair))
+                            second_product(which, chunk, pair, "second")
                             budget -= 1
 
-        for k, (b, jc) in enumerate(steps):
-            best = stronger(b, jc)
-            done_before = side[:rounded_so_far]
-            count = per_step[k] if k < len(per_step) else 0
-            for job in side[rounded_so_far : rounded_so_far + count]:
-                round_weight("scalar", job[0], job[1], job[2], job[3])
-            rounded_so_far += count
+        pending = None
+        for k, (b, step) in enumerate(steps):
+            best = stronger_load(b, step)
+            if pending is not None:
+                less_relief(*pending, False)
+            pending = (b, step, best)
+            if GPSIMD_FROM <= k < len(steps) - 1 and step % 2 == 1:
+                less_relief(*pending, True)
+                pending = None
+            if k < len(pieces):
+                n, g, q0, q1 = pieces[k]
+                round_weight(nc.scalar.copy, late_raw[n, g][:, :, PACK * q0 : PACK * q1], n, g, q0, q1)
             if k == 1:
-                nc.scalar.copy(out=deal(w1_c[:].bitcast(U16))[:, 1], in_=undealt(w1_raw[:].bitcast(U16))[:, 1])
-            if k == 4:
-                deal_scales(wa_c, wa_raw)
-            if k == 12:
-                nc.scalar.copy(out=gc_wide[:], in_=gc_t[:].unsqueeze(2).to_broadcast([P, PACK, M_FIRST]))
-            second_stage(3)
-            if before is not None:
-                less_relief(*before)
-            if k >= 2 and steps[k - 2][1] % 2 == 1:
-                b2, jc2 = steps[k - 2]
-                quantise_h(b2, jc2 // 2)
-                if b2 == 1:
-                    ready_chunks.append(jc2 // 2)
-            for n, g, q0, q1 in done_before:
-                if q1 == P and (n, g) not in quantised:
-                    quantised.add((n, g))
-                    quantise_weight(n, g)
-            before = (k, b, jc, best)
-        less_relief(*before)
-        second_stage(16)
-        last = S // QC - 1
+                deal_w1_words(1)
+            second_stage(BANKS_PER_STEP, k > len(pieces))
+            if k >= 1 and steps[k - 1][1] % 2 == 1:
+                b_done, step_done = steps[k - 1]
+                quantise_h(b_done, step_done // 2)
+                if b_done == 1:
+                    ready_chunks.append(step_done // 2)
+            if 1 <= k <= len(pieces) and pieces[k - 1][3] == P:
+                quantise_weight(*pieces[k - 1][:2])
+        less_relief(*pending, False)
+        second_stage(4 * CHUNKS, True)
+        last = CHUNKS - 1
         quantise_h(1, last)
         for pair in range(2):
-            for which in ("e", "d"):
-                second_product(which, last, pair, "w2" if which == "e" else "w1")
+            second_product("e", last, pair, "w2")
+            second_product("d", last, pair, "w1")
 
         out_rows = out_0.rearrange("(p t) m -> p t m", t=PACK)
         out_words = out_1[0].rearrange("p m t -> p (m t)").bitcast(I32)
-        doors = [held("doors%d" % t, [P, P_OUT], F32) for t in range(PACK)]
+        doors = [held("doors%d" % t, [P, M], F32) for t in range(PACK)]
         for t in range(PACK):
             col = slice(t, t + 1)
-            nc.scalar.activation(out=bias_t[:, col], in_=top[:, last, col], func=ACT.Copy, scale=ntemp_t[:, col])
+            nc.scalar.activation(out=bias_t[:, col], in_=top[:, last, col], func=ACT.Copy, scale=minus_temp[:, col])
             nc.scalar.activation(
                 out=doors[t][:], in_=e_t[t][:].indirect(pos1_t[:]), func=ACT.Exp,
                 bias=bias_t[:, col], scale=temp_t[:, col],
@@ -308,42 +308,38 @@ def tile_list_dock_door_desk_kernel(
         def lanes_of(t, m0, m1):
             lanes = ring.tile([P, m1 - m0], F32, name="lanes")
             nc.vector.tensor_tensor(
-                out=lanes[:], in0=d_t[t][:].indirect(pos2_t[:, m0 // 16 : m1 // 16]),
+                out=lanes[:], in0=d_t[t][:].indirect(pos2_t[:, m0 // PER_COLUMN : m1 // PER_COLUMN]),
                 in1=gc_wide[:, t, : m1 - m0], op=ALU.mult,
             )
             return lanes
 
-        parts = ((0, M_FIRST), (M_FIRST, P_OUT))
+        parts = ((0, M_FIRST), (M_FIRST, M))
         jobs = [(t, m0, m1) for m0, m1 in parts for t in range(PACK)]
         y = {m0: held("y%d" % m0, [P, PACK, m1 - m0], F32) for m0, m1 in parts}
         y_bf = {m0: held("y_bf%d" % m0, [P, PACK * (m1 - m0)], BF16) for m0, m1 in parts}
 
-        def weave(m0, m1):
+        def store_and_weave(m0, m1):
             nc.sync.dma_start(out=out_rows[:, :, m0:m1], in_=y[m0][:])
-            src = y[m0][:].rearrange("p t (c i) -> p c t i", i=4)
-            dst = y_bf[m0][:].rearrange("p (c i t) -> p c t i", i=4, t=PACK)
-            if m0 == 0:
-                nc.scalar.copy(out=dst, in_=src)
-            else:
-                nc.vector.tensor_copy(out=dst, in_=src)
-
-        def planes(m0, m1):
-            nc.vector.quantize_mx(out=y_c[:, m0:m1].bitcast(E4M3), scales=y_s[:, m0:m1], in_=y_bf[m0][:])
-            nc.sync.dma_start(out=out_words[:, m0:m1], in_=y_c[:, m0:m1])
+            copy = nc.scalar.copy if m0 == 0 else nc.vector.tensor_copy
+            copy(
+                out=y_bf[m0][:].rearrange("p (c i t) -> p c t i", i=4, t=PACK),
+                in_=y[m0][:].rearrange("p t (c i) -> p c t i", i=4),
+            )
 
         ahead = lanes_of(*jobs[0])
-        for n, (t, m0, m1) in enumerate(jobs):
+        for index, (t, m0, m1) in enumerate(jobs):
             lanes = ahead
-            if n + 1 < len(jobs):
-                ahead = lanes_of(*jobs[n + 1])
+            if index + 1 < len(jobs):
+                ahead = lanes_of(*jobs[index + 1])
             nc.vector.scalar_tensor_tensor(
                 out=y[m0][:, t, :], in0=doors[t][:, m0:m1], scalar=ga_t[:, t : t + 1], in1=lanes[:],
                 op0=ALU.mult, op1=ALU.max,
             )
             if t == PACK - 1:
-                weave(m0, m1)
+                store_and_weave(m0, m1)
         for m0, m1 in parts:
-            planes(m0, m1)
+            nc.vector.quantize_mx(out=y_c[:, m0:m1].bitcast(E4M3), scales=y_s[:, m0:m1], in_=y_bf[m0][:])
+            nc.sync.dma_start(out=out_words[:, m0:m1], in_=y_c[:, m0:m1])
         for q in range(4):
             queue = nc.sync if q % 2 else nc.scalar
-            queue.dma_start(out=out_2[0, 4 * q : 4 * q + 4, :].bitcast(I32), in_=y_s[32 * q : 32 * q + 4, :].bitcast(I32))
+            queue.dma_start(out=out_2[0, 4 * q : 4 * q + 4, :].bitcast(I32), in_=scale_rows(y_s, q))

@@ -41,8 +41,8 @@ def tile_list_dock_door_desk_kernel(
         ring = ctx.enter_context(tc.tile_pool(name="ring", bufs=3))
         psum = ctx.enter_context(tc.psum_pool(name="psum", bufs=2))
 
-        def held(name, shape, dtype):
-            return keep.tile(shape, dtype, name=name, align_bytes=64)
+        def held(name, shape, dtype, tag=None):
+            return keep.tile(shape, dtype, name=name, tag=tag or name, align_bytes=64)
 
         offs_t = held("offs_t", [P, S // PER_COLUMN], U16)
         pos1_t = held("pos1_t", [P, M // PER_COLUMN], U16)
@@ -52,7 +52,7 @@ def tile_list_dock_door_desk_kernel(
         v_w = held("v_w", [P, S], U32)
         v_s = held("v_s", [P, S], U8)
         w1_raw = held("w1_raw", [P, 2 * H], U8)
-        w1_sraw = held("w1_sraw", [P, H], U8)
+        w1_sraw = held("w1_sraw", [P, H], U8, tag="w2_s")
         w1_c = held("w1_c", [P, 2 * H], U8)
         w1_s = held("w1_s", [P, H], U8)
         wa_raw = held("wa_raw", [P, 2 * N], I32)
@@ -104,11 +104,11 @@ def tile_list_dock_door_desk_kernel(
         nc.sync.dma_start(offs_t[:], offs)
         nc.sync.dma_start(out=tab_w[:], in_=tab_words[0].rearrange("p c i -> p (c i)").bitcast(I32))
         load_scales(tab_s, tab_scales[0])
+        nc.sync.dma_start(out=w1_raw[:].bitcast(I32), in_=w1_words[0].bitcast(I32))
         load_early("w2", 0)
         load_early("w2", 1)
-        nc.sync.dma_start(out=w1_raw[:].bitcast(I32), in_=w1_words[0].bitcast(I32))
-        load_early("w3", 0)
         load_scales(w1_sraw, w1_scales[0])
+        load_early("w3", 0)
         load_early("w3", 1)
         load_rows(late_raw["w2", 1], w2[:, PASS:])
         load_rows(late_raw["w3", 1], w3[:, PASS:])
@@ -180,7 +180,7 @@ def tile_list_dock_door_desk_kernel(
         def stronger_load(b, step):
             load1 = ring.tile([P, PACK * STEP], F32, name="load1")
             nc.scalar.activation(out=woven(load1[:]), in_=first_product("w1", b, step), func=ACT.Copy)
-            best = ring.tile([P, PACK * STEP], F32, name="best")
+            best = ring.tile([P, PACK * STEP], F32, name="best", bufs=4)
             nc.vector.tensor_tensor(out=woven(best[:]), in0=first_product("w2", b, step), in1=woven(load1[:]), op=ALU.max)
             return best
 
@@ -232,9 +232,9 @@ def tile_list_dock_door_desk_kernel(
         gather_table(0)
         round_weight(nc.scalar.copy, early_raw["w2", 0][:], "w2", 0, 0, P // 2)
         round_weight(nc.scalar.copy, early_raw["w2", 1][:], "w2", 0, P // 2, P)
-        quantise_weight("w2", 0)
         deal_w1_words(0)
-        nc.vector.tensor_copy(out=dealt(w1_s[:]), in_=undealt(w1_sraw[:]))
+        deal_on_gpsimd(w1_s, w1_sraw)
+        quantise_weight("w2", 0)
         gather_table(1)
         round_weight(nc.scalar.copy, early_raw["w3", 0][:], "w3", 0, 0, P // 2)
         round_weight(nc.vector.tensor_copy, early_raw["w3", 1][:], "w3", 0, P // 2, P)
@@ -264,29 +264,34 @@ def tile_list_dock_door_desk_kernel(
                             second_product(which, chunk, pair, "second")
                             budget -= 1
 
-        pending = None
+        bests = []
+
+        def subtract(k):
+            less_relief(*steps[k], bests[k], k >= GPSIMD_FROM and k % 2 == 1)
+
+        def close_chunk(k):
+            b_done, step_done = steps[k]
+            quantise_h(b_done, step_done // 2)
+            if b_done == 1:
+                ready_chunks.append(step_done // 2)
+
         for k, (b, step) in enumerate(steps):
-            best = stronger_load(b, step)
-            if pending is not None:
-                less_relief(*pending, False)
-            pending = (b, step, best)
-            if GPSIMD_FROM <= k < len(steps) - 1 and step % 2 == 1:
-                less_relief(*pending, True)
-                pending = None
+            bests.append(stronger_load(b, step))
             if k < len(pieces):
                 n, g, q0, q1 = pieces[k]
                 round_weight(nc.scalar.copy, late_raw[n, g][:, :, PACK * q0 : PACK * q1], n, g, q0, q1)
             if k == 1:
                 deal_w1_words(1)
             second_stage(BANKS_PER_STEP, k > len(pieces))
-            if k >= 1 and steps[k - 1][1] % 2 == 1:
-                b_done, step_done = steps[k - 1]
-                quantise_h(b_done, step_done // 2)
-                if b_done == 1:
-                    ready_chunks.append(step_done // 2)
+            if k >= 3 and k % 2 == 0:
+                close_chunk(k - 3)
+            if k >= 2:
+                subtract(k - 2)
             if 1 <= k <= len(pieces) and pieces[k - 1][3] == P:
                 quantise_weight(*pieces[k - 1][:2])
-        less_relief(*pending, False)
+        close_chunk(len(steps) - 3)
+        subtract(len(steps) - 2)
+        subtract(len(steps) - 1)
         second_stage(4 * CHUNKS, True)
         last = CHUNKS - 1
         quantise_h(1, last)

from contextlib import ExitStack

import concourse.mybir as mybir

K, H, N, T, S, M = 512, 1024, 512, 2048, 1024, 512
FLOPS = 2 * 3 * K * H * S + 2 * 2 * H * N * S

F32 = mybir.dt.float32
BF16 = mybir.dt.bfloat16
I32 = mybir.dt.int32
U32 = mybir.dt.uint32
U16 = mybir.dt.uint16
U8 = mybir.dt.uint8
E4M3 = mybir.dt.float8_e4m3fn_x4
E2M1 = mybir.dt.float4_e2m1fn_x4
ALU = mybir.AluOpType
ACT = mybir.ActivationFunctionType

P = 128
PACK = 4
PASS = P * PACK
PER_COLUMN = 16
STEP = 128
CHUNK = 2 * STEP
CHUNKS = S // CHUNK
LEAD = 2.5
PIECES_FIRST_STAGE = 2
PIECES_WB = 3
GPSIMD_FROM = 8
BANKS_PER_STEP = 3
M_FIRST = 384


def tile_list_dock_door_desk_kernel(
    tc, tab_words, tab_scales, offs, pos1, pos2, w1_words, w1_scales, w2, w3,
    wa_words, wa_scales, wb, temp, ga, gc, out_0, out_1, out_2,
):
    nc = tc.nc
    with ExitStack() as ctx:
        keep = ctx.enter_context(tc.tile_pool(name="keep", bufs=1))
        ring = ctx.enter_context(tc.tile_pool(name="ring", bufs=3))
        psum = ctx.enter_context(tc.psum_pool(name="psum", bufs=2))

        def held(name, shape, dtype, tag=None):
            return keep.tile(shape, dtype, name=name, tag=tag or name, align_bytes=64)

        offs_t = held("offs_t", [P, S // PER_COLUMN], U16)
        pos1_t = held("pos1_t", [P, M // PER_COLUMN], U16)
        pos2_t = held("pos2_t", [P, M // PER_COLUMN], U16)
        tab_w = held("tab_w", [P, T], I32)
        tab_s = held("tab_s", [P, T], U8)
        v_w = held("v_w", [P, S], U32)
        v_s = held("v_s", [P, S], U8)
        w1_raw = held("w1_raw", [P, 2 * H], U8)
        w1_sraw = held("w1_sraw", [P, H], U8, tag="w2_s")
        w1_c = held("w1_c", [P, 2 * H], U8)
        w1_s = held("w1_s", [P, H], U8)
        wa_raw = held("wa_raw", [P, 2 * N], I32)
        wa_sraw = held("wa_sraw", [P, 2 * N], U8)
        wa_c = held("wa_c", [P, 2 * N], I32)
        wa_s = held("wa_s", [P, 2 * N], U8)
        float_weights = ("w2", "w3", "wb")
        late_groups = (("w2", 1), ("w3", 1), ("wb", 0), ("wb", 1))
        early_raw = {
            (n, u): held(n + "_early%d" % u, [P, PACK, PASS // 2], F32) for n in ("w2", "w3") for u in range(2)
        }
        late_raw = {(n, g): held(n + "_late%d" % g, [P, PACK, PASS], F32) for n, g in late_groups}
        rounded = {(n, g): held(n + "_bf%d" % g, [P, PACK * PASS], BF16) for n in float_weights for g in range(2)}
        codes = {n: held(n + "_c", [P, 2 * PASS], U32) for n in float_weights}
        scales = {n: held(n + "_s", [P, 2 * PASS], U8) for n in float_weights}
        h_c = [held("h_c%d" % b, [P, S], U32) for b in range(2)]
        h_s = [held("h_s%d" % b, [P, S], U8) for b in range(2)]
        e_t = [held("e%d" % t, [P, S], F32) for t in range(PACK)]
        d_t = [held("d%d" % t, [P, S], F32) for t in range(PACK)]
        temp_t = held("temp_t", [P, PACK], F32)
        minus_temp = held("minus_temp", [P, PACK], F32)
        ga_t = held("ga_t", [P, PACK], F32)
        gc_t = held("gc_t", [P, PACK], F32)
        gc_wide = held("gc_wide", [P, PACK, M_FIRST], F32)
        top = held("top", [P, CHUNKS, PACK], F32)
        bias_t = held("bias_t", [P, PACK], F32)
        y_c = held("y_c", [P, M], I32)
        y_s = held("y_s", [P, M], U8)

        def scale_rows(plane, q):
            return plane[32 * q : 32 * q + 4, :].bitcast(I32)

        def load_scales(plane, rows):
            for q in range(4):
                nc.sync.dma_start(out=scale_rows(plane, q), in_=rows[4 * q : 4 * q + 4, :].bitcast(I32))

        def load_rows(dst, src):
            nc.sync.dma_start(out=dst[:], in_=src.rearrange("(p i) c -> p i c", i=PACK))

        def load_early(n, u):
            load_rows(early_raw[n, u], (w2 if n == "w2" else w3)[:, u * PASS // 2 : (u + 1) * PASS // 2])

        def load_vector(dst, vec):
            nc.sync.dma_start(out=dst[:], in_=vec.rearrange("(p t) -> p t", t=PACK))

        for plane in (tab_s, w1_sraw, wa_sraw):
            nc.gpsimd.memset(plane[:].bitcast(I32), 0)
        load_vector(gc_t, gc)
        nc.sync.dma_start(offs_t[:], offs)
        nc.sync.dma_start(out=tab_w[:], in_=tab_words[0].rearrange("p c i -> p (c i)").bitcast(I32))
        load_scales(tab_s, tab_scales[0])
        nc.sync.dma_start(out=w1_raw[:].bitcast(I32), in_=w1_words[0].bitcast(I32))
        load_early("w2", 0)
        load_early("w2", 1)
        load_scales(w1_sraw, w1_scales[0])
        load_early("w3", 0)
        load_early("w3", 1)
        load_rows(late_raw["w2", 1], w2[:, PASS:])
        load_rows(late_raw["w3", 1], w3[:, PASS:])
        nc.sync.dma_start(
            out=wa_raw[:].rearrange("p (a c) -> p a c", a=2),
            in_=wa_words.rearrange("a p c i -> p a (c i)").bitcast(I32),
        )
        for q in range(4):
            nc.sync.dma_start(
                out=scale_rows(wa_sraw, q).rearrange("r (a c) -> r a c", a=2),
                in_=wa_scales[:, 4 * q : 4 * q + 4, :].bitcast(I32).rearrange("a r c -> r a c"),
            )
        load_rows(late_raw["wb", 0], wb[:PASS, :])
        load_rows(late_raw["wb", 1], wb[PASS:, :])
        nc.sync.dma_start(pos1_t[:], pos1)
        nc.sync.dma_start(pos2_t[:], pos2)
        load_vector(temp_t, temp)
        load_vector(ga_t, ga)

        def gather_table(half):
            cols = slice(half * S // 2, (half + 1) * S // 2)
            entries = offs_t[:, cols.start // PER_COLUMN : cols.stop // PER_COLUMN]
            nc.vector.tensor_copy(out=v_w[:, cols], in_=tab_w[:].bitcast(U32).indirect(entries))
            nc.vector.tensor_copy(out=v_s[:, cols], in_=tab_s[:].indirect(entries))

        def dealt(ap):
            return ap.rearrange("p (g t q) -> p g q t", g=2, t=PACK)

        def undealt(ap):
            return ap.rearrange("p (g q t) -> p g q t", g=2, t=PACK)

        def deal_w1_words(g):
            nc.scalar.copy(out=dealt(w1_c[:].bitcast(U16))[:, g], in_=undealt(w1_raw[:].bitcast(U16))[:, g])

        def deal_on_gpsimd(dst, src):
            for g in range(2):
                cols = slice(g * PASS, (g + 1) * PASS)
                nc.gpsimd.tensor_copy(
                    out=dst[:, cols].rearrange("p (t q) -> p t q", t=PACK),
                    in_=src[:, cols].rearrange("p (q t) -> p t q", t=PACK),
                )

        def round_weight(copy, raw, n, g, q0, q1):
            dst = rounded[n, g][:].rearrange("p (t q i) -> p q i t", t=PACK, i=PACK)[:, q0:q1]
            copy(out=dst, in_=raw.rearrange("p i (q t) -> p q i t", t=PACK))

        def quantise_weight(n, g):
            cols = slice(g * PASS, (g + 1) * PASS)
            nc.vector.quantize_mx(out=codes[n][:, cols].bitcast(E4M3), scales=scales[n][:, cols], in_=rounded[n, g][:])

        def first_product(n, b, step):
            bank = psum.tile([P, PACK * STEP], F32, name="bank_" + n)
            js = slice(step * STEP, (step + 1) * STEP)
            for t in range(PACK):
                c0 = b * PASS + t * P
                if n == "w1":
                    lhs, lhs_s = w1_c[:, 2 * c0 : 2 * (c0 + P)].bitcast(E2M1), w1_s[:, c0 : c0 + P]
                else:
                    lhs, lhs_s = codes[n][:, c0 : c0 + P].bitcast(E4M3), scales[n][:, c0 : c0 + P]
                nc.tensor.matmul_mx(
                    out=bank[:, t * STEP : (t + 1) * STEP], lhsT=lhs, lhsT_scale=lhs_s,
                    rhs=v_w[:, js].bitcast(E4M3), rhs_scale=v_s[:, js], start=True, stop=True,
                )
            return bank[:].rearrange("p (t j) -> p j t", t=PACK)

        def woven(ap):
            return ap.rearrange("p (j t) -> p j t", t=PACK)

        def stronger_load(b, step):
            load1 = ring.tile([P, PACK * STEP], F32, name="load1")
            nc.scalar.activation(out=woven(load1[:]), in_=first_product("w1", b, step), func=ACT.Copy)
            best = ring.tile([P, PACK * STEP], F32, name="best", bufs=4)
            nc.vector.tensor_tensor(out=woven(best[:]), in0=first_product("w2", b, step), in1=woven(load1[:]), op=ALU.max)
            return best

        h_bf = {}

        def less_relief(b, step, best, on_gpsimd):
            chunk, part = divmod(step, 2)
            if part == 0:
                h_bf[b, chunk] = ring.tile([P, PACK * CHUNK], BF16, name="h_bf", align_bytes=64, bufs=4)
            dst = h_bf[b, chunk][:, part * PACK * STEP : (part + 1) * PACK * STEP]
            if on_gpsimd:
                relief = ring.tile([P, PACK * STEP], F32, name="relief")
                nc.scalar.activation(out=woven(relief[:]), in_=first_product("w3", b, step), func=ACT.Copy)
                nc.gpsimd.tensor_tensor(out=dst, in0=best[:], in1=relief[:], op=ALU.subtract)
            else:
                nc.vector.tensor_tensor(
                    out=woven(dst), in0=woven(best[:]), in1=first_product("w3", b, step), op=ALU.subtract,
                )

        def quantise_h(b, chunk):
            cols = slice(chunk * CHUNK, (chunk + 1) * CHUNK)
            nc.vector.quantize_mx(out=h_c[b][:, cols].bitcast(E4M3), scales=h_s[b][:, cols], in_=h_bf[b, chunk][:])

        def second_product(which, chunk, pair, tag):
            bank = psum.tile([P, 2 * CHUNK], F32, name="bank_" + tag)
            cols = slice(chunk * CHUNK, (chunk + 1) * CHUNK)
            w_c, w_s = (wa_c, wa_s) if which == "e" else (codes["wb"], scales["wb"])
            for u in range(2):
                for a in range(2):
                    c0 = a * PASS + (2 * pair + u) * P
                    nc.tensor.matmul_mx(
                        out=bank[:, u * CHUNK : (u + 1) * CHUNK],
                        lhsT=w_c[:, c0 : c0 + P].bitcast(E4M3), lhsT_scale=w_s[:, c0 : c0 + P],
                        rhs=h_c[a][:, cols].bitcast(E4M3), rhs_scale=h_s[a][:, cols],
                        start=(a == 0), stop=(a == 1),
                    )
            for u in range(2):
                t = 2 * pair + u
                src = bank[:, u * CHUNK : (u + 1) * CHUNK]
                if which == "e":
                    so_far = None if chunk == 0 else top[:, chunk - 1, t : t + 1]
                    nc.vector.tensor_scalar(
                        out=e_t[t][:, cols], in0=src, scalar1=1.0, scalar2=so_far,
                        op0=ALU.mult, op1=ALU.max, accum_out=top[:, chunk, t : t + 1],
                    )
                else:
                    nc.scalar.activation(out=d_t[t][:, cols], in_=src, func=ACT.Copy)

        gather_table(0)
        round_weight(nc.scalar.copy, early_raw["w2", 0][:], "w2", 0, 0, P // 2)
        round_weight(nc.scalar.copy, early_raw["w2", 1][:], "w2", 0, P // 2, P)
        deal_w1_words(0)
        deal_on_gpsimd(w1_s, w1_sraw)
        quantise_weight("w2", 0)
        gather_table(1)
        round_weight(nc.scalar.copy, early_raw["w3", 0][:], "w3", 0, 0, P // 2)
        round_weight(nc.vector.tensor_copy, early_raw["w3", 1][:], "w3", 0, P // 2, P)
        quantise_weight("w3", 0)

        deal_on_gpsimd(wa_s, wa_sraw)
        nc.gpsimd.tensor_scalar(out=minus_temp[:], in0=temp_t[:], scalar1=-1.0, scalar2=0.0, op0=ALU.mult, op1=ALU.add)
        for t in range(PACK):
            nc.gpsimd.tensor_copy(out=gc_wide[:, t, :], in_=gc_t[:, t : t + 1].to_broadcast([P, M_FIRST]))
        deal_on_gpsimd(wa_c, wa_raw)

        steps = sorted(((b, step) for b in range(2) for step in range(S // STEP)), key=lambda s: s[1] // 2 + LEAD * s[0])
        pieces = []
        for n, g in late_groups:
            count = PIECES_WB if n == "wb" else PIECES_FIRST_STAGE
            bounds = [2 * (u * P // 2 // count) for u in range(count + 1)]
            pieces.extend((n, g, bounds[u], bounds[u + 1]) for u in range(count))
        ready_chunks = []
        issued = set()

        def second_stage(budget, wb_ready):
            for chunk in ready_chunks:
                for pair in range(2):
                    for which in ("e", "d"):
                        if budget and (which, chunk, pair) not in issued and (which == "e" or wb_ready):
                            issued.add((which, chunk, pair))
                            second_product(which, chunk, pair, "second")
                            budget -= 1

        bests = []

        def subtract(k):
            less_relief(*steps[k], bests[k], k >= GPSIMD_FROM and k % 2 == 1)

        def close_chunk(k):
            b_done, step_done = steps[k]
            quantise_h(b_done, step_done // 2)
            if b_done == 1:
                ready_chunks.append(step_done // 2)

        for k, (b, step) in enumerate(steps):
            bests.append(stronger_load(b, step))
            if k < len(pieces):
                n, g, q0, q1 = pieces[k]
                round_weight(nc.scalar.copy, late_raw[n, g][:, :, PACK * q0 : PACK * q1], n, g, q0, q1)
            if k == 1:
                deal_w1_words(1)
            second_stage(BANKS_PER_STEP, k > len(pieces))
            if k >= 3 and k % 2 == 0:
                close_chunk(k - 3)
            if k >= 2:
                subtract(k - 2)
            if 1 <= k <= len(pieces) and pieces[k - 1][3] == P:
                quantise_weight(*pieces[k - 1][:2])
        close_chunk(len(steps) - 3)
        subtract(len(steps) - 2)
        subtract(len(steps) - 1)
        second_stage(4 * CHUNKS, True)
        last = CHUNKS - 1
        quantise_h(1, last)
        for pair in range(2):
            second_product("e", last, pair, "w2")
            second_product("d", last, pair, "w1")

        out_rows = out_0.rearrange("(p t) m -> p t m", t=PACK)
        out_words = out_1[0].rearrange("p m t -> p (m t)").bitcast(I32)
        doors = [held("doors%d" % t, [P, M], F32) for t in range(PACK)]
        for t in range(PACK):
            col = slice(t, t + 1)
            nc.scalar.activation(out=bias_t[:, col], in_=top[:, last, col], func=ACT.Copy, scale=minus_temp[:, col])
            nc.scalar.activation(
                out=doors[t][:], in_=e_t[t][:].indirect(pos1_t[:]), func=ACT.Exp,
                bias=bias_t[:, col], scale=temp_t[:, col],
            )

        def lanes_of(t, m0, m1):
            lanes = ring.tile([P, m1 - m0], F32, name="lanes")
            nc.vector.tensor_tensor(
                out=lanes[:], in0=d_t[t][:].indirect(pos2_t[:, m0 // PER_COLUMN : m1 // PER_COLUMN]),
                in1=gc_wide[:, t, : m1 - m0], op=ALU.mult,
            )
            return lanes

        parts = ((0, M_FIRST), (M_FIRST, M))
        jobs = [(t, m0, m1) for m0, m1 in parts for t in range(PACK)]
        y = {m0: held("y%d" % m0, [P, PACK, m1 - m0], F32) for m0, m1 in parts}
        y_bf = {m0: held("y_bf%d" % m0, [P, PACK * (m1 - m0)], BF16) for m0, m1 in parts}

        def store_and_weave(m0, m1):
            nc.sync.dma_start(out=out_rows[:, :, m0:m1], in_=y[m0][:])
            copy = nc.scalar.copy if m0 == 0 else nc.vector.tensor_copy
            copy(
                out=y_bf[m0][:].rearrange("p (c i t) -> p c t i", i=4, t=PACK),
                in_=y[m0][:].rearrange("p t (c i) -> p c t i", i=4),
            )

        ahead = lanes_of(*jobs[0])
        for index, (t, m0, m1) in enumerate(jobs):
            lanes = ahead
            if index + 1 < len(jobs):
                ahead = lanes_of(*jobs[index + 1])
            nc.vector.scalar_tensor_tensor(
                out=y[m0][:, t, :], in0=doors[t][:, m0:m1], scalar=ga_t[:, t : t + 1], in1=lanes[:],
                op0=ALU.mult, op1=ALU.max,
            )
            if t == PACK - 1:
                store_and_weave(m0, m1)
        for m0, m1 in parts:
            nc.vector.quantize_mx(out=y_c[:, m0:m1].bitcast(E4M3), scales=y_s[:, m0:m1], in_=y_bf[m0][:])
            nc.sync.dma_start(out=out_words[:, m0:m1], in_=y_c[:, m0:m1])
        for q in range(4):
            queue = nc.sync if q % 2 else nc.scalar
            queue.dma_start(out=out_2[0, 4 * q : 4 * q + 4, :].bitcast(I32), in_=scale_rows(y_s, q))
